import numpy as np
import ml_dtypes


def mxq(x, axis, fmt="e4m3"):
    dtype, down = {"e4m3": (ml_dtypes.float8_e4m3fn, 7), "e5m2": (ml_dtypes.float8_e5m2, 14)}[fmt]
    v = np.moveaxis(np.asarray(x, np.float32).astype(ml_dtypes.bfloat16).astype(np.float64), axis, -1)
    blocks = v.reshape(v.shape[:-1] + (-1, 32))
    amax = np.abs(blocks).max(-1, keepdims=True)
    byte = np.maximum(np.where(amax > 0, np.frexp(amax)[1] - 1 + 127, 0) - down, 1)
    scale = np.exp2(byte - 127.0)
    codes = (blocks / scale).astype(np.float32).astype(dtype).astype(np.float64)
    return np.moveaxis((codes * scale).reshape(v.shape), -1, axis)


WIDE = False


def mx_kscale(k):
    if not WIDE:
        return np.ones(k)
    levels = np.array([10, -10, 5, -5, 0])
    if k % 512:
        return np.exp2(np.random.permutation(np.resize(levels, k // 32))).repeat(32)
    a = np.empty((k // 512, 16))
    for p in range(k // 512):
        a[p, :8] = np.random.permutation(np.resize(levels, 8))
        for g in range(8):
            far = levels[np.abs(levels - a[p, g]) >= 10]
            a[p, g + 8] = far[np.random.randint(len(far))]
    return np.exp2(a.ravel()).repeat(32)


def f64(x):
    return np.asarray(x).astype(np.float64)


def striped(idx):
    return np.tile(np.asarray(idx).reshape(-1, 16).T, (8, 1)).astype(np.uint16)


def unstriped(offs):
    return offs[:16].T.reshape(-1).astype(np.int64)


E2M1 = np.array([0.0, 0.5, 1.0, 1.5, 2.0, 3.0, 4.0, 6.0, -0.0, -0.5, -1.0, -1.5, -2.0, -3.0, -4.0, -6.0])


def pack_weight(w, fmt):
    k, n = w.shape
    w = f64(np.asarray(w, np.float32).astype(ml_dtypes.bfloat16)).reshape(k // 32, 32, n)
    amax = np.abs(w).max(1)
    if fmt == "e4m3":
        byte = np.frexp(amax)[1] - 1 + 127 - 7
    else:
        mant, ex = np.frexp(amax / 6.0)
        byte = np.where(mant > 0.5, ex, ex - 1) + 127
    byte = np.clip(np.where(amax > 0, byte, 1), 1, 254)
    scaled = (w * np.exp2(127.0 - byte)[:, None, :]).reshape(k, n).astype(np.float32)
    by_word = np.ascontiguousarray(scaled.reshape(k // 512, 128, 4, n).transpose(0, 1, 3, 2))
    if fmt == "e4m3":
        words = by_word.astype(ml_dtypes.float8_e4m3fn).view(np.uint8)
    else:
        c = by_word.astype(ml_dtypes.float4_e2m1fn).view(np.uint8) & 0xF
        words = (c[..., 0::2] | (c[..., 1::2] << 4)).reshape(k // 512, 128, 2 * n)
    return np.ascontiguousarray(words), np.ascontiguousarray(byte.astype(np.uint8).reshape(k // 512, 16, n))


def unpack_weight(words, scales, fmt):
    g, _, n = scales.shape
    words = np.ascontiguousarray(words).reshape(g, 128, n, -1)
    if fmt == "e4m3":
        vals = words.view(ml_dtypes.float8_e4m3fn).astype(np.float64)
    else:
        nib = np.empty((g, 128, n, 4), np.uint8)
        nib[..., 0::2] = words & 0xF
        nib[..., 1::2] = words >> 4
        vals = E2M1[nib]
    vals = vals * np.repeat(np.exp2(scales.astype(np.float64) - 127.0), 8, axis=1)[..., None]
    return vals.transpose(0, 1, 3, 2).reshape(g * 512, n)


def bf(x):
    return np.asarray(x, np.float32).astype(ml_dtypes.bfloat16)


def planes(Y):
    r, m = Y.shape
    b = f64(bf(Y)).reshape(r // 32, 32, m)
    amax = np.abs(b).max(1)
    byte = np.clip(np.where(amax > 0, np.frexp(amax)[1] - 1 + 127 - 7, 1), 1, 254)
    codes = (b * np.exp2(127.0 - byte)[:, None, :]).reshape(r, m).astype(np.float32).astype(ml_dtypes.float8_e4m3fn).view(np.uint8)
    words = codes.reshape(r // 512, 128, 4, m).transpose(0, 1, 3, 2)
    return np.ascontiguousarray(words), np.ascontiguousarray(byte.astype(np.uint8).reshape(r // 512, 16, m))


D, T, I, Q, E, K = 512, 2048, 512, 256, 512, 512


def setup_inputs():
    n = np.random.standard_normal
    idx = np.random.permutation(T)[:I]
    fd = mx_kscale(D)
    fi = mx_kscale(I)
    fk = mx_kscale(K)
    ti = np.ones(T)
    ti[idx] = fi
    keysp = pack_weight(n((D, T)) / fd[:, None], "e4m3")
    return {
        "query": (n((D, Q)) * 0.25 / np.sqrt(D) * fd[:, None]).astype(np.float32),
        "keys_words": keysp[0],
        "keys_scales": keysp[1],
        "size": (np.random.uniform(4.0, 12.0, (1, I)) * fi).astype(np.float32),
        "vals": (n((E, T)) / ti).astype(np.float32),
        "cond": (n((K, Q)) * fk[:, None]).astype(np.float32),
        "wg": (n((K, E)) * 0.5 / np.sqrt(K) / fk[:, None]).astype(np.float32),
        "wb": (n((K, E)) * 0.3 / np.sqrt(K) / fk[:, None]).astype(np.float32),
        "offs": striped(idx),
    }


def reference(query, keys_words, keys_scales, size, vals, cond, wg, wb, offs):
    idx = unstriped(offs)
    keysu = unpack_weight(keys_words, keys_scales, "e4m3")
    queryq = mxq(f64(query), 0, "e4m3")
    keysidxg = keysu[:, idx]
    a = queryq.T @ keysidxg
    p = np.exp(a - np.max(a, axis=1, keepdims=True))
    w = p * f64(size) / np.sum(p, axis=1, keepdims=True)
    wt = w.T
    vt = f64(vals)[:, idx].T
    vtq = mxq(vt, 0, "e4m3")
    wtq = mxq(wt, 0, "e4m3")
    o = vtq.T @ wtq
    wgq = mxq(f64(wg), 0, "e4m3")
    condq = mxq(f64(cond), 0, "e4m3")
    g = wgq.T @ condq
    wbq = mxq(f64(wb), 0, "e4m3")
    b = wbq.T @ condq
    y = o * (1.0 + g) + b
    words, scales = planes(y)
    return y, words, scales

@@ -1,0 +1,226 @@
+from contextlib import ExitStack
+
+import concourse.mybir as mybir
+from concourse.masks import make_identity
+
+D, T, I, Q, E, K = 512, 2048, 512, 256, 512, 512
+FLOPS = 2 * Q * (D * I + I * E + 2 * K * E)
+
+F32 = mybir.dt.float32
+BF16 = mybir.dt.bfloat16
+I32 = mybir.dt.int32
+U32 = mybir.dt.uint32
+U16 = mybir.dt.uint16
+U8 = mybir.dt.uint8
+FP8X4 = mybir.dt.float8_e4m3fn_x4
+ACT = mybir.ActivationFunctionType
+ALU = mybir.AluOpType
+AXIS = mybir.AxisListType
+
+P = 128
+PACK = 4
+HALVES = Q // P
+
+
+def tile_attend_filmattn_pl_kernel(tc, query, keys_words, keys_scales, size, vals, cond, wg, wb, offs,
+                                    out_0, out_1, out_2):
+    nc = tc.nc
+    with ExitStack() as ctx:
+        keep = ctx.enter_context(tc.tile_pool(name="keep", bufs=1))
+        psum = ctx.enter_context(tc.psum_pool(name="psum", bufs=2))
+
+        def sb(name, shape, dtype, after=None):
+            return keep.tile(shape, dtype, name=name, tag=after or name, align_bytes=64)
+
+        def by_four(rows):
+            return rows.rearrange("(p t) c -> p t c", t=PACK)
+
+        def quantise(name, grouped, width, after=None):
+            codes = sb(name + "_codes", [P, width], I32, after)
+            scales = sb(name + "_scales", [P, width], U8)
+            nc.vector.quantize_mx(out=codes[:].bitcast(FP8X4), scales=scales[:], in_=grouped)
+            return codes, scales
+
+        def product(out, lhs, lhs_cols, rhs):
+            nc.tensor.matmul_mx(out=out, lhsT=lhs[0][:, lhs_cols].bitcast(FP8X4), lhsT_scale=lhs[1][:, lhs_cols],
+                                rhs=rhs[0][:].bitcast(FP8X4), rhs_scale=rhs[1][:], start=True, stop=True)
+
+        def interleave(copy, name, raw, width):
+            grouped = sb(name + "_grouped", [P, width * PACK], BF16)
+            copy(grouped[:].rearrange("p (c i t) -> p c t i", i=4, t=PACK),
+                 raw.rearrange("p t (c i) -> p c t i", i=4))
+            return grouped
+
+        def deal(name, raw, on_scalar):
+            grouped = sb(name + "_grouped", [P, E * PACK], BF16)
+            dst = grouped[:].rearrange("p (j m t) -> p m t j", j=PACK, t=PACK)
+            src = raw.rearrange("p t (m j) -> p m t j", j=PACK)
+            if on_scalar:
+                nc.scalar.copy(dst[:, :on_scalar], src[:, :on_scalar])
+            nc.vector.tensor_copy(dst[:, on_scalar:], src[:, on_scalar:])
+            return grouped
+
+        offsets = keep.tile([P, I // 16], U16, name="offsets")
+        key_bytes = sb("key_bytes", [P, T], U8)
+        nc.gpsimd.memset(key_bytes[:].bitcast(I32), 0)
+        ident = sb("ident", [P, P], F32)
+        make_identity(nc, ident[:])
+
+        query_raw = sb("query_raw", [P, PACK, Q], F32)
+        key_words = sb("key_words", [P, T], I32)
+        size_cols = sb("size_cols", [P, PACK], F32)
+        cond_raw = sb("cond_raw", [P, PACK, Q], F32)
+        wg_raw = sb("wg_raw", [P, PACK, E], F32)
+        wb_raw = sb("wb_raw", [P, PACK, E], F32)
+        val_rows = [sb("val_rows%d" % j, [P, T], F32) for j in range(PACK)]
+
+        nc.sync.dma_start(offsets[:], offs)
+        nc.sync.dma_start(query_raw[:], by_four(query))
+        for quad in range(4):
+            nc.sync.dma_start(key_bytes[32 * quad:32 * quad + 4, :].bitcast(I32),
+                              keys_scales[0, 4 * quad:4 * quad + 4, :].bitcast(I32))
+        nc.sync.dma_start(key_words[:], keys_words[0].rearrange("p c r -> p (c r)").bitcast(I32))
+        nc.sync.dma_start(size_cols[:], size.rearrange("o (p t) -> (o p) t", t=PACK))
+        nc.sync.dma_start(cond_raw[:], by_four(cond))
+        nc.sync.dma_start(val_rows[0][:], by_four(vals)[:, 0, :])
+        nc.sync.dma_start(wg_raw[:], by_four(wg))
+        nc.sync.dma_start(val_rows[1][:], by_four(vals)[:, 1, :])
+        nc.sync.dma_start(wb_raw[:], by_four(wb))
+        nc.sync.dma_start(val_rows[2][:], by_four(vals)[:, 2, :])
+        nc.sync.dma_start(val_rows[3][:], by_four(vals)[:, 3, :])
+
+        warm = sb("warm", [P, 2], F32)
+        nc.vector.memset(warm[:, 0:1], 0.0)
+        nc.scalar.activation(warm[:, 1:2], warm[:, 0:1], ACT.Exp)
+
+        query_grouped = interleave(nc.scalar.copy, "query", query_raw[:], Q)
+        picked_bytes = sb("picked_bytes", [P, I], U8)
+        nc.vector.tensor_copy(picked_bytes[:], key_bytes[:].indirect(offsets[:]))
+        query_q = quantise("query", query_grouped[:], Q)
+        picked_words = sb("picked_words", [P, I], U32)
+        nc.vector.tensor_copy(picked_words[:], key_words[:].bitcast(U32).indirect(offsets[:]))
+        keys_q = (picked_words, picked_bytes)
+
+        size_rows = psum.tile([P, PACK, P], F32, tag="turn", name="size_rows")
+        for t in range(PACK):
+            nc.tensor.transpose(size_rows[:, t, :], size_cols[:, t:t + 1].to_broadcast([P, P]), ident[:])
+
+        scores = []
+        for h in range(HALVES):
+            bank = psum.tile([P, I], F32, tag="acc", name="scores%d" % h)
+            product(bank[:], query_q, slice(h * P, (h + 1) * P), keys_q)
+            scores.append(bank)
+
+        cond_grouped = interleave(nc.scalar.copy, "cond", cond_raw[:], Q)
+
+        neg_max = [sb("neg_max%d" % h, [P, 1], F32) for h in range(HALVES)]
+        row_sum = [sb("row_sum%d" % h, [P, 1], F32) for h in range(HALVES)]
+        inv_sum = [sb("inv_sum%d" % h, [P, 1], F32) for h in range(HALVES)]
+        expd = [sb("expd%d" % h, [P, I], F32, "cond_raw" if h == 0 else None) for h in range(HALVES)]
+        for h in range(HALVES):
+            nc.vector.tensor_reduce(neg_max[h][:], scores[h][:], AXIS.X, ALU.max, negate=True)
+            nc.scalar.activation(expd[h][:], scores[h][:], ACT.Exp, bias=neg_max[h][:], accum_out=row_sum[h][:])
+        cond_q = quantise("cond", cond_grouped[:], Q)
+
+        def gather(j):
+            picked = sb("picked_vals%d" % j, [P, I], BF16)
+            nc.vector.tensor_copy(picked[:], val_rows[j][:].indirect(offsets[:]))
+            turned = psum.tile([P, 2, P], F32, tag="turn", name="turned_v%d" % j)
+            pairs = picked[:].bitcast(F32)
+            for u in range(2):
+                nc.tensor.transpose(turned[:, u, :], pairs[:, u:I // 2:2], ident[:])
+            grouped = sb("v_grouped%d" % j, [P, P * PACK], BF16)
+            nc.scalar.copy(grouped[:].bitcast(F32).rearrange("p (e u) -> p e u", u=2),
+                           turned[:].rearrange("p u e -> p e u"))
+            return grouped
+
+        grouped0 = gather(0)
+        weights = sb("weights", [P, HALVES, I], BF16, "val_rows0")
+        for h in range(HALVES):
+            nc.vector.reciprocal(inv_sum[h][:], row_sum[h][:])
+            nc.vector.scalar_tensor_tensor(
+                weights[:, h, :].rearrange("p (n t) -> p n t", t=PACK),
+                expd[h][:].rearrange("p (n t) -> p n t", t=PACK), inv_sum[h][:],
+                size_rows[:].rearrange("p t n -> p n t"), ALU.mult, ALU.mult)
+
+        turned_w = psum.tile([P, HALVES, 2, P], F32, tag="turn", name="turned_w")
+        for h in range(HALVES):
+            pairs = weights[:, h, :].bitcast(F32)
+            for u in range(2):
+                nc.tensor.transpose(turned_w[:, h, u, :], pairs[:, u:I // 2:2], ident[:])
+
+        wg_grouped = deal("wg", wg_raw[:], 64)
+
+        w_grouped = sb("w_grouped", [P, Q * PACK], BF16, "wg_raw")
+        nc.scalar.copy(w_grouped[:].bitcast(F32).rearrange("p (h q u) -> p h q u", h=HALVES, u=2),
+                       turned_w[:].rearrange("p h u q -> p h q u"))
+        wg_q = quantise("wg", wg_grouped[:], E)
+
+        def project(name, weight_q):
+            banks = [psum.tile([P, 2, Q], F32, tag=name, name="%s%d" % (name, b)) for b in range(2)]
+            for j in range(PACK):
+                product(banks[j // 2][:, j % 2, :], weight_q, slice(j * P, (j + 1) * P), cond_q)
+            return banks
+
+        gain_banks = project("gain", wg_q)
+        gain = sb("gain", [P, PACK, Q], F32)
+        for b in range(2):
+            nc.scalar.activation(gain[:, 2 * b:2 * b + 2, :], gain_banks[b][:], ACT.Copy, bias=1.0)
+
+        def attend(j, v_q):
+            bank = psum.tile([P, Q], F32, tag="acc", name="attended%d" % j)
+            product(bank[:], v_q, slice(0, P), w_q)
+            return bank
+
+        def scale(j, bank, scaled, pieces):
+            for cols in pieces:
+                nc.vector.tensor_tensor(scaled[:, cols], bank[:, cols], gain[:, j, cols], ALU.mult)
+
+        def shift(j, scaled, pieces):
+            for cols in pieces:
+                nc.vector.tensor_tensor(result[:, j, cols], scaled[:, cols], shift_banks[j // 2][:, j % 2, cols],
+                                        ALU.add)
+
+        every = [slice(0, Q)]
+        halves = [slice(h * P, (h + 1) * P) for h in range(HALVES)]
+        v0_q = quantise("v0", grouped0[:], P)
+        grouped1 = gather(1)
+        w_q = quantise("w", w_grouped[:], Q, "val_rows1")
+        bank0 = attend(0, v0_q)
+        wb_grouped = deal("wb", wb_raw[:], 32)
+        bank1 = attend(1, quantise("v1", grouped1[:], P, "wb_raw"))
+        wb_q = quantise("wb", wb_grouped[:], E)
+        scaled0 = sb("scaled0", [P, Q], F32, "wb_grouped")
+        scale(0, bank0, scaled0[:], every)
+        shift_banks = project("shift", wb_q)
+        grouped2 = gather(2)
+        result = sb("result", [P, PACK, Q], F32, "val_rows2")
+        scale(1, bank1, result[:, 1, :], every)
+        shift(0, scaled0[:], every)
+        shift(1, result[:, 1, :], every)
+        grouped3 = gather(3)
+        bank2 = attend(2, quantise("v2", grouped2[:], P, "val_rows3"))
+        bank3 = attend(3, quantise("v3", grouped3[:], P))
+        scaled2 = sb("scaled2", [P, Q], F32, "v_grouped3")
+        scale(2, bank2, scaled2[:], every)
+        shift(2, scaled2[:], every)
+        nc.sync.dma_start(by_four(out_0)[:, 0:3, :], result[:, 0:3, :])
+        scale(3, bank3, result[:, 3, :], halves)
+        shift(3, result[:, 3, :], halves)
+        nc.sync.dma_start(by_four(out_0)[:, 3, :], result[:, 3, :])
+
+        y_grouped = sb("y_grouped", [P, Q * PACK], BF16)
+        y_codes = sb("y_codes", [P, Q], I32)
+        y_scales = sb("y_scales", [P, Q], U8)
+        for h in range(HALVES):
+            nc.vector.tensor_copy(
+                y_grouped[:, h * P * PACK:(h + 1) * P * PACK].rearrange("p (c i t) -> p c t i", i=4, t=PACK),
+                result[:, :, halves[h]].rearrange("p t (c i) -> p c t i", i=4))
+        for h in range(HALVES):
+            nc.vector.quantize_mx(out=y_codes[:, halves[h]].bitcast(FP8X4), scales=y_scales[:, halves[h]],
+                                  in_=y_grouped[:, h * P * PACK:(h + 1) * P * PACK])
+        nc.sync.dma_start(out_1[0].rearrange("p c r -> p (c r)").bitcast(I32), y_codes[:])
+        for quad in range(4):
+            queue = nc.scalar if quad % 2 else nc.sync
+            queue.dma_start(out_2[0, 4 * quad:4 * quad + 4, :].bitcast(I32),
+                            y_scales[32 * quad:32 * quad + 4, :].bitcast(I32))

@@ -35,15 +35,17 @@ def tile_attend_filmattn_pl_kernel(tc, query, keys_words, keys_scales, size, val
         def by_four(rows):
             return rows.rearrange("(p t) c -> p t c", t=PACK)
 
+        def quantise_into(name, grouped, codes):
+            scales = sb(name + "_scales", [P, codes.shape[1]], U8)
+            nc.vector.quantize_mx(out=codes.bitcast(FP8X4), scales=scales[:], in_=grouped)
+            return codes, scales[:]
+
         def quantise(name, grouped, width, after=None):
-            codes = sb(name + "_codes", [P, width], I32, after)
-            scales = sb(name + "_scales", [P, width], U8)
-            nc.vector.quantize_mx(out=codes[:].bitcast(FP8X4), scales=scales[:], in_=grouped)
-            return codes, scales
+            return quantise_into(name, grouped, sb(name + "_codes", [P, width], I32, after)[:])
 
         def product(out, lhs, lhs_cols, rhs):
             nc.tensor.matmul_mx(out=out, lhsT=lhs[0][:, lhs_cols].bitcast(FP8X4), lhsT_scale=lhs[1][:, lhs_cols],
-                                rhs=rhs[0][:].bitcast(FP8X4), rhs_scale=rhs[1][:], start=True, stop=True)
+                                rhs=rhs[0].bitcast(FP8X4), rhs_scale=rhs[1], start=True, stop=True)
 
         def interleave(copy, name, raw, width):
             grouped = sb(name + "_grouped", [P, width * PACK], BF16)
@@ -51,13 +53,13 @@ def tile_attend_filmattn_pl_kernel(tc, query, keys_words, keys_scales, size, val
                  raw.rearrange("p t (c i) -> p c t i", i=4))
             return grouped
 
-        def deal(name, raw, on_scalar):
+        def deal(copies, name, raw):
             grouped = sb(name + "_grouped", [P, E * PACK], BF16)
             dst = grouped[:].rearrange("p (j m t) -> p m t j", j=PACK, t=PACK)
             src = raw.rearrange("p t (m j) -> p m t j", j=PACK)
-            if on_scalar:
-                nc.scalar.copy(dst[:, :on_scalar], src[:, :on_scalar])
-            nc.vector.tensor_copy(dst[:, on_scalar:], src[:, on_scalar:])
+            share = P // len(copies)
+            for n, copy in enumerate(copies):
+                copy(dst[:, n * share:(n + 1) * share], src[:, n * share:(n + 1) * share])
             return grouped
 
         offsets = keep.tile([P, I // 16], U16, name="offsets")
@@ -89,17 +91,13 @@ def tile_attend_filmattn_pl_kernel(tc, query, keys_words, keys_scales, size, val
         nc.sync.dma_start(val_rows[2][:], by_four(vals)[:, 2, :])
         nc.sync.dma_start(val_rows[3][:], by_four(vals)[:, 3, :])
 
-        warm = sb("warm", [P, 2], F32)
-        nc.vector.memset(warm[:, 0:1], 0.0)
-        nc.scalar.activation(warm[:, 1:2], warm[:, 0:1], ACT.Exp)
-
-        query_grouped = interleave(nc.scalar.copy, "query", query_raw[:], Q)
+        query_grouped = interleave(lambda dst, src: nc.scalar.activation(dst, src, ACT.Copy), "query", query_raw[:], Q)
         picked_bytes = sb("picked_bytes", [P, I], U8)
         nc.vector.tensor_copy(picked_bytes[:], key_bytes[:].indirect(offsets[:]))
-        query_q = quantise("query", query_grouped[:], Q)
+        query_q = quantise("query", query_grouped[:], Q, "key_bytes")
         picked_words = sb("picked_words", [P, I], U32)
         nc.vector.tensor_copy(picked_words[:], key_words[:].bitcast(U32).indirect(offsets[:]))
-        keys_q = (picked_words, picked_bytes)
+        keys_q = (picked_words[:], picked_bytes[:])
 
         size_rows = psum.tile([P, PACK, P], F32, tag="turn", name="size_rows")
         for t in range(PACK):
@@ -114,12 +112,11 @@ def tile_attend_filmattn_pl_kernel(tc, query, keys_words, keys_scales, size, val
         cond_grouped = interleave(nc.scalar.copy, "cond", cond_raw[:], Q)
 
         neg_max = [sb("neg_max%d" % h, [P, 1], F32) for h in range(HALVES)]
-        row_sum = [sb("row_sum%d" % h, [P, 1], F32) for h in range(HALVES)]
-        inv_sum = [sb("inv_sum%d" % h, [P, 1], F32) for h in range(HALVES)]
+        row_sum = sb("row_sum", [P, HALVES], F32)
         expd = [sb("expd%d" % h, [P, I], F32, "cond_raw" if h == 0 else None) for h in range(HALVES)]
         for h in range(HALVES):
             nc.vector.tensor_reduce(neg_max[h][:], scores[h][:], AXIS.X, ALU.max, negate=True)
-            nc.scalar.activation(expd[h][:], scores[h][:], ACT.Exp, bias=neg_max[h][:], accum_out=row_sum[h][:])
+            nc.scalar.activation(expd[h][:], scores[h][:], ACT.Exp, bias=neg_max[h][:], accum_out=row_sum[:, h:h + 1])
         cond_q = quantise("cond", cond_grouped[:], Q)
 
         def gather(j):
@@ -135,12 +132,13 @@ def tile_attend_filmattn_pl_kernel(tc, query, keys_words, keys_scales, size, val
             return grouped
 
         grouped0 = gather(0)
-        weights = sb("weights", [P, HALVES, I], BF16, "val_rows0")
+        weights = sb("weights", [P, HALVES, I], BF16)
+        inv_sum = sb("inv_sum", [P, HALVES], F32, "val_rows0")
+        nc.vector.reciprocal(inv_sum[:], row_sum[:])
         for h in range(HALVES):
-            nc.vector.reciprocal(inv_sum[h][:], row_sum[h][:])
             nc.vector.scalar_tensor_tensor(
                 weights[:, h, :].rearrange("p (n t) -> p n t", t=PACK),
-                expd[h][:].rearrange("p (n t) -> p n t", t=PACK), inv_sum[h][:],
+                expd[h][:].rearrange("p (n t) -> p n t", t=PACK), inv_sum[:, h:h + 1],
                 size_rows[:].rearrange("p t n -> p n t"), ALU.mult, ALU.mult)
 
         turned_w = psum.tile([P, HALVES, 2, P], F32, tag="turn", name="turned_w")
@@ -149,12 +147,16 @@ def tile_attend_filmattn_pl_kernel(tc, query, keys_words, keys_scales, size, val
             for u in range(2):
                 nc.tensor.transpose(turned_w[:, h, u, :], pairs[:, u:I // 2:2], ident[:])
 
-        wg_grouped = deal("wg", wg_raw[:], 64)
+        wg_grouped = deal([nc.scalar.copy], "wg", wg_raw[:])
 
         w_grouped = sb("w_grouped", [P, Q * PACK], BF16, "wg_raw")
         nc.scalar.copy(w_grouped[:].bitcast(F32).rearrange("p (h q u) -> p h q u", h=HALVES, u=2),
                        turned_w[:].rearrange("p h u q -> p h q u"))
-        wg_q = quantise("wg", wg_grouped[:], E)
+        v0_q = quantise("v0", grouped0[:], P)
+        grouped1 = gather(1)
+        late_codes = sb("late_codes", [P, E + Q], I32, "val_rows1")
+        wg_q = quantise_into("wg", wg_grouped[:], late_codes[:, :E])
+        w_q = quantise_into("w", w_grouped[:], late_codes[:, E:])
 
         def project(name, weight_q):
             banks = [psum.tile([P, 2, Q], F32, tag=name, name="%s%d" % (name, b)) for b in range(2)]
@@ -163,59 +165,43 @@ def tile_attend_filmattn_pl_kernel(tc, query, keys_words, keys_scales, size, val
             return banks
 
         gain_banks = project("gain", wg_q)
-        gain = sb("gain", [P, PACK, Q], F32)
+
+        halves = [slice(h * P, (h + 1) * P) for h in range(HALVES)]
+        attended01 = psum.tile([P, 2, Q], F32, tag="acc", name="attended01")
+        product(attended01[:, 0, :], v0_q, slice(0, P), w_q)
+        product(attended01[:, 1, :], quantise("v1", grouped1[:], P), slice(0, P), w_q)
+        wb_q = quantise("wb", deal([nc.scalar.copy, nc.vector.tensor_copy], "wb", wb_raw[:])[:], E)
+        gain = sb("gain", [P, PACK, Q], F32, "wb_raw")
         for b in range(2):
             nc.scalar.activation(gain[:, 2 * b:2 * b + 2, :], gain_banks[b][:], ACT.Copy, bias=1.0)
-
-        def attend(j, v_q):
-            bank = psum.tile([P, Q], F32, tag="acc", name="attended%d" % j)
-            product(bank[:], v_q, slice(0, P), w_q)
-            return bank
-
-        def scale(j, bank, scaled, pieces):
-            for cols in pieces:
-                nc.vector.tensor_tensor(scaled[:, cols], bank[:, cols], gain[:, j, cols], ALU.mult)
-
-        def shift(j, scaled, pieces):
-            for cols in pieces:
-                nc.vector.tensor_tensor(result[:, j, cols], scaled[:, cols], shift_banks[j // 2][:, j % 2, cols],
-                                        ALU.add)
-
-        every = [slice(0, Q)]
-        halves = [slice(h * P, (h + 1) * P) for h in range(HALVES)]
-        v0_q = quantise("v0", grouped0[:], P)
-        grouped1 = gather(1)
-        w_q = quantise("w", w_grouped[:], Q, "val_rows1")
-        bank0 = attend(0, v0_q)
-        wb_grouped = deal("wb", wb_raw[:], 32)
-        bank1 = attend(1, quantise("v1", grouped1[:], P, "wb_raw"))
-        wb_q = quantise("wb", wb_grouped[:], E)
-        scaled0 = sb("scaled0", [P, Q], F32, "wb_grouped")
-        scale(0, bank0, scaled0[:], every)
         shift_banks = project("shift", wb_q)
         grouped2 = gather(2)
-        result = sb("result", [P, PACK, Q], F32, "val_rows2")
-        scale(1, bank1, result[:, 1, :], every)
-        shift(0, scaled0[:], every)
-        shift(1, result[:, 1, :], every)
+        scaled01 = sb("scaled01", [P, 2, Q], F32, "val_rows2")
+        nc.vector.tensor_tensor(scaled01[:], attended01[:], gain[:, 0:2, :], ALU.mult)
         grouped3 = gather(3)
-        bank2 = attend(2, quantise("v2", grouped2[:], P, "val_rows3"))
-        bank3 = attend(3, quantise("v3", grouped3[:], P))
+        attended2 = psum.tile([P, Q], F32, tag="acc", name="attended2")
+        product(attended2[:], quantise("v2", grouped2[:], P, "val_rows3"), slice(0, P), w_q)
+        result = sb("result", [P, PACK, Q], F32, "v_grouped2")
+        nc.vector.tensor_tensor(result[:, 0:2, :], scaled01[:], shift_banks[0][:], ALU.add)
+        y_grouped = sb("y_grouped", [P, Q * PACK], BF16)
+        y_places = y_grouped[:].rearrange("p (c t) -> p c t", t=PACK)
+        nc.scalar.copy(y_places[:, :, 0:2], result[:, 0:2, :].rearrange("p t c -> p c t"))
+        attended3 = psum.tile([P, Q], F32, tag="acc", name="attended3")
+        product(attended3[:], quantise("v3", grouped3[:], P), slice(0, P), w_q)
         scaled2 = sb("scaled2", [P, Q], F32, "v_grouped3")
-        scale(2, bank2, scaled2[:], every)
-        shift(2, scaled2[:], every)
+        nc.vector.tensor_tensor(scaled2[:], attended2[:], gain[:, 2, :], ALU.mult)
+        nc.vector.tensor_tensor(result[:, 2, :], scaled2[:], shift_banks[1][:, 0, :], ALU.add)
         nc.sync.dma_start(by_four(out_0)[:, 0:3, :], result[:, 0:3, :])
-        scale(3, bank3, result[:, 3, :], halves)
-        shift(3, result[:, 3, :], halves)
+        for cols in halves:
+            nc.vector.tensor_tensor(result[:, 3, cols], attended3[:, cols], gain[:, 3, cols], ALU.mult)
+        for cols in halves:
+            nc.vector.tensor_tensor(result[:, 3, cols], result[:, 3, cols], shift_banks[1][:, 1, cols], ALU.add)
         nc.sync.dma_start(by_four(out_0)[:, 3, :], result[:, 3, :])
 
-        y_grouped = sb("y_grouped", [P, Q * PACK], BF16)
         y_codes = sb("y_codes", [P, Q], I32)
         y_scales = sb("y_scales", [P, Q], U8)
         for h in range(HALVES):
-            nc.vector.tensor_copy(
-                y_grouped[:, h * P * PACK:(h + 1) * P * PACK].rearrange("p (c i t) -> p c t i", i=4, t=PACK),
-                result[:, :, halves[h]].rearrange("p t (c i) -> p c t i", i=4))
+            nc.vector.tensor_copy(y_places[:, halves[h], 2:4], result[:, 2:4, halves[h]].rearrange("p t c -> p c t"))
         for h in range(HALVES):
             nc.vector.quantize_mx(out=y_codes[:, halves[h]].bitcast(FP8X4), scales=y_scales[:, halves[h]],
                                   in_=y_grouped[:, h * P * PACK:(h + 1) * P * PACK])

@@ -19,7 +19,12 @@ AXIS = mybir.AxisListType
 
 P = 128
 PACK = 4
+PAIRS = PACK // 2
+QUADRANT = 32
+BLOCKS = 16
+LINE = 4
 HALVES = Q // P
+WB_ON_SCALAR = P // 2
 
 
 def tile_attend_filmattn_pl_kernel(tc, query, keys_words, keys_scales, size, vals, cond, wg, wb, offs,
@@ -28,11 +33,13 @@ def tile_attend_filmattn_pl_kernel(tc, query, keys_words, keys_scales, size, val
     with ExitStack() as ctx:
         keep = ctx.enter_context(tc.tile_pool(name="keep", bufs=1))
         psum = ctx.enter_context(tc.psum_pool(name="psum", bufs=2))
+        halves = [slice(h * P, (h + 1) * P) for h in range(HALVES)]
+        whole = slice(0, P)
 
-        def sb(name, shape, dtype, after=None):
-            return keep.tile(shape, dtype, name=name, tag=after or name, align_bytes=64)
+        def sb(name, shape, dtype, reuses=None):
+            return keep.tile(shape, dtype, name=name, tag=reuses or name, align_bytes=64)
 
-        def by_four(rows):
+        def by_place(rows):
             return rows.rearrange("(p t) c -> p t c", t=PACK)
 
         def quantise_into(name, grouped, codes):
@@ -40,27 +47,23 @@ def tile_attend_filmattn_pl_kernel(tc, query, keys_words, keys_scales, size, val
             nc.vector.quantize_mx(out=codes.bitcast(FP8X4), scales=scales[:], in_=grouped)
             return codes, scales[:]
 
-        def quantise(name, grouped, width, after=None):
-            return quantise_into(name, grouped, sb(name + "_codes", [P, width], I32, after)[:])
+        def quantise(name, grouped, width, reuses=None):
+            return quantise_into(name, grouped, sb(name + "_codes", [P, width], I32, reuses)[:])
 
         def product(out, lhs, lhs_cols, rhs):
             nc.tensor.matmul_mx(out=out, lhsT=lhs[0][:, lhs_cols].bitcast(FP8X4), lhsT_scale=lhs[1][:, lhs_cols],
                                 rhs=rhs[0].bitcast(FP8X4), rhs_scale=rhs[1], start=True, stop=True)
 
-        def interleave(copy, name, raw, width):
-            grouped = sb(name + "_grouped", [P, width * PACK], BF16)
-            copy(grouped[:].rearrange("p (c i t) -> p c t i", i=4, t=PACK),
-                 raw.rearrange("p t (c i) -> p c t i", i=4))
+        def interleave(copy, name, raw):
+            grouped = sb(name + "_grouped", [P, Q * PACK], BF16)
+            copy(grouped[:].rearrange("p (c i t) -> p c t i", i=LINE, t=PACK),
+                 raw.rearrange("p t (c i) -> p c t i", i=LINE))
             return grouped
 
-        def deal(copies, name, raw):
+        def dealt_views(name, raw):
             grouped = sb(name + "_grouped", [P, E * PACK], BF16)
-            dst = grouped[:].rearrange("p (j m t) -> p m t j", j=PACK, t=PACK)
-            src = raw.rearrange("p t (m j) -> p m t j", j=PACK)
-            share = P // len(copies)
-            for n, copy in enumerate(copies):
-                copy(dst[:, n * share:(n + 1) * share], src[:, n * share:(n + 1) * share])
-            return grouped
+            return (grouped, grouped[:].rearrange("p (j m t) -> p m t j", j=PACK, t=PACK),
+                    raw.rearrange("p t (m j) -> p m t j", j=PACK))
 
         offsets = keep.tile([P, I // 16], U16, name="offsets")
         key_bytes = sb("key_bytes", [P, T], U8)
@@ -76,25 +79,25 @@ def tile_attend_filmattn_pl_kernel(tc, query, keys_words, keys_scales, size, val
         wb_raw = sb("wb_raw", [P, PACK, E], F32)
         val_rows = [sb("val_rows%d" % j, [P, T], F32) for j in range(PACK)]
 
+        nc.sync.dma_start(query_raw[:], by_place(query))
         nc.sync.dma_start(offsets[:], offs)
-        nc.sync.dma_start(query_raw[:], by_four(query))
-        for quad in range(4):
-            nc.sync.dma_start(key_bytes[32 * quad:32 * quad + 4, :].bitcast(I32),
-                              keys_scales[0, 4 * quad:4 * quad + 4, :].bitcast(I32))
+        for r in range(PACK):
+            nc.sync.dma_start(key_bytes[r:P:QUADRANT, :].bitcast(I32),
+                              keys_scales[0, r:BLOCKS:PACK, :].bitcast(I32))
         nc.sync.dma_start(key_words[:], keys_words[0].rearrange("p c r -> p (c r)").bitcast(I32))
         nc.sync.dma_start(size_cols[:], size.rearrange("o (p t) -> (o p) t", t=PACK))
-        nc.sync.dma_start(cond_raw[:], by_four(cond))
-        nc.sync.dma_start(val_rows[0][:], by_four(vals)[:, 0, :])
-        nc.sync.dma_start(wg_raw[:], by_four(wg))
-        nc.sync.dma_start(val_rows[1][:], by_four(vals)[:, 1, :])
-        nc.sync.dma_start(wb_raw[:], by_four(wb))
-        nc.sync.dma_start(val_rows[2][:], by_four(vals)[:, 2, :])
-        nc.sync.dma_start(val_rows[3][:], by_four(vals)[:, 3, :])
+        nc.sync.dma_start(cond_raw[:], by_place(cond))
+        nc.sync.dma_start(val_rows[0][:], by_place(vals)[:, 0, :])
+        nc.sync.dma_start(wg_raw[:], by_place(wg))
+        nc.sync.dma_start(val_rows[1][:], by_place(vals)[:, 1, :])
+        nc.sync.dma_start(wb_raw[:], by_place(wb))
+        nc.sync.dma_start(val_rows[2][:], by_place(vals)[:, 2, :])
+        nc.sync.dma_start(val_rows[3][:], by_place(vals)[:, 3, :])
 
-        query_grouped = interleave(lambda dst, src: nc.scalar.activation(dst, src, ACT.Copy), "query", query_raw[:], Q)
+        query_grouped = interleave(lambda dst, src: nc.scalar.activation(dst, src, ACT.Copy), "query", query_raw[:])
         picked_bytes = sb("picked_bytes", [P, I], U8)
         nc.vector.tensor_copy(picked_bytes[:], key_bytes[:].indirect(offsets[:]))
-        query_q = quantise("query", query_grouped[:], Q, "key_bytes")
+        query_q = quantise("query", query_grouped[:], Q, reuses="key_bytes")
         picked_words = sb("picked_words", [P, I], U32)
         nc.vector.tensor_copy(picked_words[:], key_words[:].bitcast(U32).indirect(offsets[:]))
         keys_q = (picked_words[:], picked_bytes[:])
@@ -106,34 +109,37 @@ def tile_attend_filmattn_pl_kernel(tc, query, keys_words, keys_scales, size, val
         scores = []
         for h in range(HALVES):
             bank = psum.tile([P, I], F32, tag="acc", name="scores%d" % h)
-            product(bank[:], query_q, slice(h * P, (h + 1) * P), keys_q)
+            product(bank[:], query_q, halves[h], keys_q)
             scores.append(bank)
 
-        cond_grouped = interleave(nc.scalar.copy, "cond", cond_raw[:], Q)
+        cond_grouped = interleave(nc.scalar.copy, "cond", cond_raw[:])
 
         neg_max = [sb("neg_max%d" % h, [P, 1], F32) for h in range(HALVES)]
         row_sum = sb("row_sum", [P, HALVES], F32)
-        expd = [sb("expd%d" % h, [P, I], F32, "cond_raw" if h == 0 else None) for h in range(HALVES)]
+        expd = [sb("expd0", [P, I], F32, reuses="cond_raw"), sb("expd1", [P, I], F32)]
         for h in range(HALVES):
             nc.vector.tensor_reduce(neg_max[h][:], scores[h][:], AXIS.X, ALU.max, negate=True)
             nc.scalar.activation(expd[h][:], scores[h][:], ACT.Exp, bias=neg_max[h][:], accum_out=row_sum[:, h:h + 1])
         cond_q = quantise("cond", cond_grouped[:], Q)
 
+        def turn(bank, rows):
+            words = rows.bitcast(F32)
+            for u in range(PAIRS):
+                nc.tensor.transpose(bank[:, u, :], words[:, u:I // 2:PAIRS], ident[:])
+
         def gather(j):
             picked = sb("picked_vals%d" % j, [P, I], BF16)
             nc.vector.tensor_copy(picked[:], val_rows[j][:].indirect(offsets[:]))
-            turned = psum.tile([P, 2, P], F32, tag="turn", name="turned_v%d" % j)
-            pairs = picked[:].bitcast(F32)
-            for u in range(2):
-                nc.tensor.transpose(turned[:, u, :], pairs[:, u:I // 2:2], ident[:])
+            turned = psum.tile([P, PAIRS, P], F32, tag="turn", name="turned_v%d" % j)
+            turn(turned[:], picked[:])
             grouped = sb("v_grouped%d" % j, [P, P * PACK], BF16)
-            nc.scalar.copy(grouped[:].bitcast(F32).rearrange("p (e u) -> p e u", u=2),
-                           turned[:].rearrange("p u e -> p e u"))
+            nc.scalar.copy(grouped[:].bitcast(F32).rearrange("p (m u) -> p m u", u=PAIRS),
+                           turned[:].rearrange("p u m -> p m u"))
             return grouped
 
-        grouped0 = gather(0)
+        v0_grouped = gather(0)
         weights = sb("weights", [P, HALVES, I], BF16)
-        inv_sum = sb("inv_sum", [P, HALVES], F32, "val_rows0")
+        inv_sum = sb("inv_sum", [P, HALVES], F32, reuses="val_rows0")
         nc.vector.reciprocal(inv_sum[:], row_sum[:])
         for h in range(HALVES):
             nc.vector.scalar_tensor_tensor(
@@ -141,22 +147,21 @@ def tile_attend_filmattn_pl_kernel(tc, query, keys_words, keys_scales, size, val
                 expd[h][:].rearrange("p (n t) -> p n t", t=PACK), inv_sum[:, h:h + 1],
                 size_rows[:].rearrange("p t n -> p n t"), ALU.mult, ALU.mult)
 
-        turned_w = psum.tile([P, HALVES, 2, P], F32, tag="turn", name="turned_w")
+        turned_w = psum.tile([P, HALVES, PAIRS, P], F32, tag="turn", name="turned_w")
         for h in range(HALVES):
-            pairs = weights[:, h, :].bitcast(F32)
-            for u in range(2):
-                nc.tensor.transpose(turned_w[:, h, u, :], pairs[:, u:I // 2:2], ident[:])
+            turn(turned_w[:, h, :, :], weights[:, h, :])
 
-        wg_grouped = deal([nc.scalar.copy], "wg", wg_raw[:])
+        wg_grouped, wg_dst, wg_src = dealt_views("wg", wg_raw[:])
+        nc.scalar.copy(wg_dst, wg_src)
 
-        w_grouped = sb("w_grouped", [P, Q * PACK], BF16, "wg_raw")
-        nc.scalar.copy(w_grouped[:].bitcast(F32).rearrange("p (h q u) -> p h q u", h=HALVES, u=2),
+        w_grouped = sb("w_grouped", [P, Q * PACK], BF16, reuses="wg_raw")
+        nc.scalar.copy(w_grouped[:].bitcast(F32).rearrange("p (h q u) -> p h q u", h=HALVES, u=PAIRS),
                        turned_w[:].rearrange("p h u q -> p h q u"))
-        v0_q = quantise("v0", grouped0[:], P)
-        grouped1 = gather(1)
-        late_codes = sb("late_codes", [P, E + Q], I32, "val_rows1")
-        wg_q = quantise_into("wg", wg_grouped[:], late_codes[:, :E])
-        w_q = quantise_into("w", w_grouped[:], late_codes[:, E:])
+        v0_q = quantise("v0", v0_grouped[:], P)
+        v1_grouped = gather(1)
+        wg_and_w_codes = sb("wg_and_w_codes", [P, E + Q], I32, reuses="val_rows1")
+        wg_q = quantise_into("wg", wg_grouped[:], wg_and_w_codes[:, :E])
+        w_q = quantise_into("w", w_grouped[:], wg_and_w_codes[:, E:])
 
         def project(name, weight_q):
             banks = [psum.tile([P, 2, Q], F32, tag=name, name="%s%d" % (name, b)) for b in range(2)]
@@ -166,47 +171,51 @@ def tile_attend_filmattn_pl_kernel(tc, query, keys_words, keys_scales, size, val
 
         gain_banks = project("gain", wg_q)
 
-        halves = [slice(h * P, (h + 1) * P) for h in range(HALVES)]
         attended01 = psum.tile([P, 2, Q], F32, tag="acc", name="attended01")
-        product(attended01[:, 0, :], v0_q, slice(0, P), w_q)
-        product(attended01[:, 1, :], quantise("v1", grouped1[:], P), slice(0, P), w_q)
-        wb_q = quantise("wb", deal([nc.scalar.copy, nc.vector.tensor_copy], "wb", wb_raw[:])[:], E)
-        gain = sb("gain", [P, PACK, Q], F32, "wb_raw")
+        product(attended01[:, 0, :], v0_q, whole, w_q)
+        product(attended01[:, 1, :], quantise("v1", v1_grouped[:], P), whole, w_q)
+        wb_grouped, wb_dst, wb_src = dealt_views("wb", wb_raw[:])
+        nc.scalar.copy(wb_dst[:, :WB_ON_SCALAR], wb_src[:, :WB_ON_SCALAR])
+        nc.vector.tensor_copy(wb_dst[:, WB_ON_SCALAR:], wb_src[:, WB_ON_SCALAR:])
+        wb_q = quantise("wb", wb_grouped[:], E)
+        gain = sb("gain", [P, PACK, Q], F32, reuses="wb_raw")
         for b in range(2):
             nc.scalar.activation(gain[:, 2 * b:2 * b + 2, :], gain_banks[b][:], ACT.Copy, bias=1.0)
         shift_banks = project("shift", wb_q)
-        grouped2 = gather(2)
-        scaled01 = sb("scaled01", [P, 2, Q], F32, "val_rows2")
+
+        v2_grouped = gather(2)
+        scaled01 = sb("scaled01", [P, 2, Q], F32, reuses="val_rows2")
         nc.vector.tensor_tensor(scaled01[:], attended01[:], gain[:, 0:2, :], ALU.mult)
-        grouped3 = gather(3)
+        v3_grouped = gather(3)
         attended2 = psum.tile([P, Q], F32, tag="acc", name="attended2")
-        product(attended2[:], quantise("v2", grouped2[:], P, "val_rows3"), slice(0, P), w_q)
-        result = sb("result", [P, PACK, Q], F32, "v_grouped2")
+        product(attended2[:], quantise("v2", v2_grouped[:], P, reuses="val_rows3"), whole, w_q)
+        result = sb("result", [P, PACK, Q], F32, reuses="v_grouped2")
         nc.vector.tensor_tensor(result[:, 0:2, :], scaled01[:], shift_banks[0][:], ALU.add)
         y_grouped = sb("y_grouped", [P, Q * PACK], BF16)
-        y_places = y_grouped[:].rearrange("p (c t) -> p c t", t=PACK)
-        nc.scalar.copy(y_places[:, :, 0:2], result[:, 0:2, :].rearrange("p t c -> p c t"))
-        attended3 = psum.tile([P, Q], F32, tag="acc", name="attended3")
-        product(attended3[:], quantise("v3", grouped3[:], P), slice(0, P), w_q)
-        scaled2 = sb("scaled2", [P, Q], F32, "v_grouped3")
+        y_places = y_grouped[:].rearrange("p (q t) -> p q t", t=PACK)
+        nc.scalar.copy(y_places[:, :, 0:2], result[:, 0:2, :].rearrange("p t q -> p q t"))
+        v3_q = quantise("v3", v3_grouped[:], P)
+        attended3 = [psum.tile([P, P], F32, tag="gain", name="attended3_%d" % h) for h in range(HALVES)]
+        for h, cols in enumerate(halves):
+            product(attended3[h][:], v3_q, whole, (w_q[0][:, cols], w_q[1][:, cols]))
+        scaled2 = sb("scaled2", [P, Q], F32, reuses="v_grouped3")
         nc.vector.tensor_tensor(scaled2[:], attended2[:], gain[:, 2, :], ALU.mult)
         nc.vector.tensor_tensor(result[:, 2, :], scaled2[:], shift_banks[1][:, 0, :], ALU.add)
-        nc.sync.dma_start(by_four(out_0)[:, 0:3, :], result[:, 0:3, :])
-        for cols in halves:
-            nc.vector.tensor_tensor(result[:, 3, cols], attended3[:, cols], gain[:, 3, cols], ALU.mult)
+        nc.sync.dma_start(by_place(out_0)[:, 0:3, :], result[:, 0:3, :])
+        for h, cols in enumerate(halves):
+            nc.vector.tensor_tensor(result[:, 3, cols], attended3[h][:], gain[:, 3, cols], ALU.mult)
         for cols in halves:
             nc.vector.tensor_tensor(result[:, 3, cols], result[:, 3, cols], shift_banks[1][:, 1, cols], ALU.add)
-        nc.sync.dma_start(by_four(out_0)[:, 3, :], result[:, 3, :])
+        nc.sync.dma_start(by_place(out_0)[:, 3, :], result[:, 3, :])
 
         y_codes = sb("y_codes", [P, Q], I32)
         y_scales = sb("y_scales", [P, Q], U8)
-        for h in range(HALVES):
-            nc.vector.tensor_copy(y_places[:, halves[h], 2:4], result[:, 2:4, halves[h]].rearrange("p t c -> p c t"))
-        for h in range(HALVES):
-            nc.vector.quantize_mx(out=y_codes[:, halves[h]].bitcast(FP8X4), scales=y_scales[:, halves[h]],
+        for cols in halves:
+            nc.vector.tensor_copy(y_places[:, cols, 2:4], result[:, 2:4, cols].rearrange("p t q -> p q t"))
+        for h, cols in enumerate(halves):
+            nc.vector.quantize_mx(out=y_codes[:, cols].bitcast(FP8X4), scales=y_scales[:, cols],
                                   in_=y_grouped[:, h * P * PACK:(h + 1) * P * PACK])
         nc.sync.dma_start(out_1[0].rearrange("p c r -> p (c r)").bitcast(I32), y_codes[:])
-        for quad in range(4):
-            queue = nc.scalar if quad % 2 else nc.sync
-            queue.dma_start(out_2[0, 4 * quad:4 * quad + 4, :].bitcast(I32),
-                            y_scales[32 * quad:32 * quad + 4, :].bitcast(I32))
+        for r in range(PACK):
+            queue = nc.scalar if r % 2 else nc.sync
+            queue.dma_start(out_2[0, r:BLOCKS:PACK, :].bitcast(I32), y_scales[r:P:QUADRANT, :].bitcast(I32))

from contextlib import ExitStack

import concourse.mybir as mybir
from concourse.masks import make_identity

D, T, I, Q, E, K = 512, 2048, 512, 256, 512, 512
FLOPS = 2 * Q * (D * I + I * E + 2 * K * E)

F32 = mybir.dt.float32
BF16 = mybir.dt.bfloat16
I32 = mybir.dt.int32
U32 = mybir.dt.uint32
U16 = mybir.dt.uint16
U8 = mybir.dt.uint8
FP8X4 = mybir.dt.float8_e4m3fn_x4
ACT = mybir.ActivationFunctionType
ALU = mybir.AluOpType
AXIS = mybir.AxisListType

P = 128
PACK = 4
PAIRS = PACK // 2
QUADRANT = 32
BLOCKS = 16
LINE = 4
HALVES = Q // P
WB_ON_SCALAR = P // 2


def tile_attend_filmattn_pl_kernel(tc, query, keys_words, keys_scales, size, vals, cond, wg, wb, offs,
                                    out_0, out_1, out_2):
    nc = tc.nc
    with ExitStack() as ctx:
        keep = ctx.enter_context(tc.tile_pool(name="keep", bufs=1))
        psum = ctx.enter_context(tc.psum_pool(name="psum", bufs=2))
        halves = [slice(h * P, (h + 1) * P) for h in range(HALVES)]
        whole = slice(0, P)

        def sb(name, shape, dtype, reuses=None):
            return keep.tile(shape, dtype, name=name, tag=reuses or name, align_bytes=64)

        def by_place(rows):
            return rows.rearrange("(p t) c -> p t c", t=PACK)

        def quantise_into(name, grouped, codes):
            scales = sb(name + "_scales", [P, codes.shape[1]], U8)
            nc.vector.quantize_mx(out=codes.bitcast(FP8X4), scales=scales[:], in_=grouped)
            return codes, scales[:]

        def quantise(name, grouped, width, reuses=None):
            return quantise_into(name, grouped, sb(name + "_codes", [P, width], I32, reuses)[:])

        def product(out, lhs, lhs_cols, rhs):
            nc.tensor.matmul_mx(out=out, lhsT=lhs[0][:, lhs_cols].bitcast(FP8X4), lhsT_scale=lhs[1][:, lhs_cols],
                                rhs=rhs[0].bitcast(FP8X4), rhs_scale=rhs[1], start=True, stop=True)

        def interleave(copy, name, raw):
            grouped = sb(name + "_grouped", [P, Q * PACK], BF16)
            copy(grouped[:].rearrange("p (c i t) -> p c t i", i=LINE, t=PACK),
                 raw.rearrange("p t (c i) -> p c t i", i=LINE))
            return grouped

        def dealt_views(name, raw):
            grouped = sb(name + "_grouped", [P, E * PACK], BF16)
            return (grouped, grouped[:].rearrange("p (j m t) -> p m t j", j=PACK, t=PACK),
                    raw.rearrange("p t (m j) -> p m t j", j=PACK))

        offsets = keep.tile([P, I // 16], U16, name="offsets")
        key_bytes = sb("key_bytes", [P, T], U8)
        nc.gpsimd.memset(key_bytes[:].bitcast(I32), 0)
        ident = sb("ident", [P, P], F32)
        make_identity(nc, ident[:])

        query_raw = sb("query_raw", [P, PACK, Q], F32)
        key_words = sb("key_words", [P, T], I32)
        size_cols = sb("size_cols", [P, PACK], F32)
        cond_raw = sb("cond_raw", [P, PACK, Q], F32)
        wg_raw = sb("wg_raw", [P, PACK, E], F32)
        wb_raw = sb("wb_raw", [P, PACK, E], F32)
        val_rows = [sb("val_rows%d" % j, [P, T], F32) for j in range(PACK)]

        nc.sync.dma_start(query_raw[:], by_place(query))
        nc.sync.dma_start(offsets[:], offs)
        for r in range(PACK):
            nc.sync.dma_start(key_bytes[r:P:QUADRANT, :].bitcast(I32),
                              keys_scales[0, r:BLOCKS:PACK, :].bitcast(I32))
        nc.sync.dma_start(key_words[:], keys_words[0].rearrange("p c r -> p (c r)").bitcast(I32))
        nc.sync.dma_start(size_cols[:], size.rearrange("o (p t) -> (o p) t", t=PACK))
        nc.sync.dma_start(cond_raw[:], by_place(cond))
        nc.sync.dma_start(val_rows[0][:], by_place(vals)[:, 0, :])
        nc.sync.dma_start(wg_raw[:], by_place(wg))
        nc.sync.dma_start(val_rows[1][:], by_place(vals)[:, 1, :])
        nc.sync.dma_start(wb_raw[:], by_place(wb))
        nc.sync.dma_start(val_rows[2][:], by_place(vals)[:, 2, :])
        nc.sync.dma_start(val_rows[3][:], by_place(vals)[:, 3, :])

        query_grouped = interleave(lambda dst, src: nc.scalar.activation(dst, src, ACT.Copy), "query", query_raw[:])
        picked_bytes = sb("picked_bytes", [P, I], U8)
        nc.vector.tensor_copy(picked_bytes[:], key_bytes[:].indirect(offsets[:]))
        query_q = quantise("query", query_grouped[:], Q, reuses="key_bytes")
        picked_words = sb("picked_words", [P, I], U32)
        nc.vector.tensor_copy(picked_words[:], key_words[:].bitcast(U32).indirect(offsets[:]))
        keys_q = (picked_words[:], picked_bytes[:])

        size_rows = psum.tile([P, PACK, P], F32, tag="turn", name="size_rows")
        for t in range(PACK):
            nc.tensor.transpose(size_rows[:, t, :], size_cols[:, t:t + 1].to_broadcast([P, P]), ident[:])

        scores = []
        for h in range(HALVES):
            bank = psum.tile([P, I], F32, tag="acc", name="scores%d" % h)
            product(bank[:], query_q, halves[h], keys_q)
            scores.append(bank)

        cond_grouped = interleave(nc.scalar.copy, "cond", cond_raw[:])

        neg_max = [sb("neg_max%d" % h, [P, 1], F32) for h in range(HALVES)]
        row_sum = sb("row_sum", [P, HALVES], F32)
        expd = [sb("expd0", [P, I], F32, reuses="cond_raw"), sb("expd1", [P, I], F32)]
        for h in range(HALVES):
            nc.vector.tensor_reduce(neg_max[h][:], scores[h][:], AXIS.X, ALU.max, negate=True)
            nc.scalar.activation(expd[h][:], scores[h][:], ACT.Exp, bias=neg_max[h][:], accum_out=row_sum[:, h:h + 1])
        cond_q = quantise("cond", cond_grouped[:], Q)

        def turn(bank, rows):
            words = rows.bitcast(F32)
            for u in range(PAIRS):
                nc.tensor.transpose(bank[:, u, :], words[:, u:I // 2:PAIRS], ident[:])

        def gather(j):
            picked = sb("picked_vals%d" % j, [P, I], BF16)
            nc.vector.tensor_copy(picked[:], val_rows[j][:].indirect(offsets[:]))
            turned = psum.tile([P, PAIRS, P], F32, tag="turn", name="turned_v%d" % j)
            turn(turned[:], picked[:])
            grouped = sb("v_grouped%d" % j, [P, P * PACK], BF16)
            nc.scalar.copy(grouped[:].bitcast(F32).rearrange("p (m u) -> p m u", u=PAIRS),
                           turned[:].rearrange("p u m -> p m u"))
            return grouped

        v0_grouped = gather(0)
        weights = sb("weights", [P, HALVES, I], BF16)
        inv_sum = sb("inv_sum", [P, HALVES], F32, reuses="val_rows0")
        nc.vector.reciprocal(inv_sum[:], row_sum[:])
        for h in range(HALVES):
            nc.vector.scalar_tensor_tensor(
                weights[:, h, :].rearrange("p (n t) -> p n t", t=PACK),
                expd[h][:].rearrange("p (n t) -> p n t", t=PACK), inv_sum[:, h:h + 1],
                size_rows[:].rearrange("p t n -> p n t"), ALU.mult, ALU.mult)

        turned_w = psum.tile([P, HALVES, PAIRS, P], F32, tag="turn", name="turned_w")
        for h in range(HALVES):
            turn(turned_w[:, h, :, :], weights[:, h, :])

        wg_grouped, wg_dst, wg_src = dealt_views("wg", wg_raw[:])
        nc.scalar.copy(wg_dst, wg_src)

        w_grouped = sb("w_grouped", [P, Q * PACK], BF16, reuses="wg_raw")
        nc.scalar.copy(w_grouped[:].bitcast(F32).rearrange("p (h q u) -> p h q u", h=HALVES, u=PAIRS),
                       turned_w[:].rearrange("p h u q -> p h q u"))
        v0_q = quantise("v0", v0_grouped[:], P)
        v1_grouped = gather(1)
        wg_and_w_codes = sb("wg_and_w_codes", [P, E + Q], I32, reuses="val_rows1")
        wg_q = quantise_into("wg", wg_grouped[:], wg_and_w_codes[:, :E])
        w_q = quantise_into("w", w_grouped[:], wg_and_w_codes[:, E:])

        def project(name, weight_q):
            banks = [psum.tile([P, 2, Q], F32, tag=name, name="%s%d" % (name, b)) for b in range(2)]
            for j in range(PACK):
                product(banks[j // 2][:, j % 2, :], weight_q, slice(j * P, (j + 1) * P), cond_q)
            return banks

        gain_banks = project("gain", wg_q)

        attended01 = psum.tile([P, 2, Q], F32, tag="acc", name="attended01")
        product(attended01[:, 0, :], v0_q, whole, w_q)
        product(attended01[:, 1, :], quantise("v1", v1_grouped[:], P), whole, w_q)
        wb_grouped, wb_dst, wb_src = dealt_views("wb", wb_raw[:])
        nc.scalar.copy(wb_dst[:, :WB_ON_SCALAR], wb_src[:, :WB_ON_SCALAR])
        nc.vector.tensor_copy(wb_dst[:, WB_ON_SCALAR:], wb_src[:, WB_ON_SCALAR:])
        wb_q = quantise("wb", wb_grouped[:], E)
        gain = sb("gain", [P, PACK, Q], F32, reuses="wb_raw")
        for b in range(2):
            nc.scalar.activation(gain[:, 2 * b:2 * b + 2, :], gain_banks[b][:], ACT.Copy, bias=1.0)
        shift_banks = project("shift", wb_q)

        v2_grouped = gather(2)
        scaled01 = sb("scaled01", [P, 2, Q], F32, reuses="val_rows2")
        nc.vector.tensor_tensor(scaled01[:], attended01[:], gain[:, 0:2, :], ALU.mult)
        v3_grouped = gather(3)
        attended2 = psum.tile([P, Q], F32, tag="acc", name="attended2")
        product(attended2[:], quantise("v2", v2_grouped[:], P, reuses="val_rows3"), whole, w_q)
        result = sb("result", [P, PACK, Q], F32, reuses="v_grouped2")
        nc.vector.tensor_tensor(result[:, 0:2, :], scaled01[:], shift_banks[0][:], ALU.add)
        y_grouped = sb("y_grouped", [P, Q * PACK], BF16)
        y_places = y_grouped[:].rearrange("p (q t) -> p q t", t=PACK)
        nc.scalar.copy(y_places[:, :, 0:2], result[:, 0:2, :].rearrange("p t q -> p q t"))
        v3_q = quantise("v3", v3_grouped[:], P)
        attended3 = [psum.tile([P, P], F32, tag="gain", name="attended3_%d" % h) for h in range(HALVES)]
        for h, cols in enumerate(halves):
            product(attended3[h][:], v3_q, whole, (w_q[0][:, cols], w_q[1][:, cols]))
        scaled2 = sb("scaled2", [P, Q], F32, reuses="v_grouped3")
        nc.vector.tensor_tensor(scaled2[:], attended2[:], gain[:, 2, :], ALU.mult)
        nc.vector.tensor_tensor(result[:, 2, :], scaled2[:], shift_banks[1][:, 0, :], ALU.add)
        nc.sync.dma_start(by_place(out_0)[:, 0:3, :], result[:, 0:3, :])
        for h, cols in enumerate(halves):
            nc.vector.tensor_tensor(result[:, 3, cols], attended3[h][:], gain[:, 3, cols], ALU.mult)
        for cols in halves:
            nc.vector.tensor_tensor(result[:, 3, cols], result[:, 3, cols], shift_banks[1][:, 1, cols], ALU.add)
        nc.sync.dma_start(by_place(out_0)[:, 3, :], result[:, 3, :])

        y_codes = sb("y_codes", [P, Q], I32)
        y_scales = sb("y_scales", [P, Q], U8)
        for cols in halves:
            nc.vector.tensor_copy(y_places[:, cols, 2:4], result[:, 2:4, cols].rearrange("p t q -> p q t"))
        for h, cols in enumerate(halves):
            nc.vector.quantize_mx(out=y_codes[:, cols].bitcast(FP8X4), scales=y_scales[:, cols],
                                  in_=y_grouped[:, h * P * PACK:(h + 1) * P * PACK])
        nc.sync.dma_start(out_1[0].rearrange("p c r -> p (c r)").bitcast(I32), y_codes[:])
        for r in range(PACK):
            queue = nc.scalar if r % 2 else nc.sync
            queue.dma_start(out_2[0, r:BLOCKS:PACK, :].bitcast(I32), y_scales[r:P:QUADRANT, :].bitcast(I32))
